import numpy as np
import ml_dtypes


def mxq(x, axis, fmt="e4m3"):
    dtype, down = {"e4m3": (ml_dtypes.float8_e4m3fn, 7), "e5m2": (ml_dtypes.float8_e5m2, 14)}[fmt]
    v = np.moveaxis(np.asarray(x, np.float32).astype(ml_dtypes.bfloat16).astype(np.float64), axis, -1)
    blocks = v.reshape(v.shape[:-1] + (-1, 32))
    amax = np.abs(blocks).max(-1, keepdims=True)
    byte = np.maximum(np.where(amax > 0, np.frexp(amax)[1] - 1 + 127, 0) - down, 1)
    scale = np.exp2(byte - 127.0)
    codes = (blocks / scale).astype(np.float32).astype(dtype).astype(np.float64)
    return np.moveaxis((codes * scale).reshape(v.shape), -1, axis)


WIDE = False


def mx_kscale(k):
    if not WIDE:
        return np.ones(k)
    levels = np.array([10, -10, 5, -5, 0])
    if k % 512:
        return np.exp2(np.random.permutation(np.resize(levels, k // 32))).repeat(32)
    a = np.empty((k // 512, 16))
    for p in range(k // 512):
        a[p, :8] = np.random.permutation(np.resize(levels, 8))
        for g in range(8):
            far = levels[np.abs(levels - a[p, g]) >= 10]
            a[p, g + 8] = far[np.random.randint(len(far))]
    return np.exp2(a.ravel()).repeat(32)


def f64(x):
    return np.asarray(x).astype(np.float64)


def striped(idx):
    return np.tile(idx.reshape(-1, 16).T, (8, 1)).astype(np.uint16)


def unstriped(offs):
    return offs[:16].T.reshape(-1).astype(np.int64)


E2M1 = np.array([0.0, 0.5, 1.0, 1.5, 2.0, 3.0, 4.0, 6.0, -0.0, -0.5, -1.0, -1.5, -2.0, -3.0, -4.0, -6.0])


def pack_weight(w, fmt):
    k, n = w.shape
    w = f64(np.asarray(w, np.float32).astype(ml_dtypes.bfloat16)).reshape(k // 32, 32, n)
    amax = np.abs(w).max(1)
    if fmt == "e4m3":
        byte = np.frexp(amax)[1] - 1 + 127 - 7
    else:
        mant, ex = np.frexp(amax / 6.0)
        byte = np.where(mant > 0.5, ex, ex - 1) + 127
    byte = np.clip(np.where(amax > 0, byte, 1), 1, 254)
    scaled = (w * np.exp2(127.0 - byte)[:, None, :]).reshape(k, n).astype(np.float32)
    by_word = np.ascontiguousarray(scaled.reshape(k // 512, 128, 4, n).transpose(0, 1, 3, 2))
    if fmt == "e4m3":
        words = by_word.astype(ml_dtypes.float8_e4m3fn).view(np.uint8)
    else:
        c = by_word.astype(ml_dtypes.float4_e2m1fn).view(np.uint8) & 0xF
        words = (c[..., 0::2] | (c[..., 1::2] << 4)).reshape(k // 512, 128, 2 * n)
    return np.ascontiguousarray(words), np.ascontiguousarray(byte.astype(np.uint8).reshape(k // 512, 16, n))


def unpack_weight(words, scales, fmt):
    g, _, n = scales.shape
    words = np.ascontiguousarray(words).reshape(g, 128, n, -1)
    if fmt == "e4m3":
        vals = words.view(ml_dtypes.float8_e4m3fn).astype(np.float64)
    else:
        nib = np.empty((g, 128, n, 4), np.uint8)
        nib[..., 0::2] = words & 0xF
        nib[..., 1::2] = words >> 4
        vals = E2M1[nib]
    vals = vals * np.repeat(np.exp2(scales.astype(np.float64) - 127.0), 8, axis=1)[..., None]
    return vals.transpose(0, 1, 3, 2).reshape(g * 512, n)


def relu(v):
    return np.maximum(v, 0.0)


def d_relu(v):
    return (v > 0).astype(np.float64)


K, T, E, C, H, N = 128, 2048, 12, 128, 512, 512


def by_expert(wq, xq):
    return np.concatenate([wq[e].T @ xq[:, e * C:(e + 1) * C] for e in range(E)], axis=1)


def setup_inputs():
    n = np.random.standard_normal
    s = mx_kscale(N)[:, None]
    u = mx_kscale(H)
    w2 = [pack_weight(m, "e2m1") for m in n((E, N, H)) / np.sqrt(N) / s[None] * u[None, None, :]]
    w1 = [pack_weight(m, "e2m1") for m in n((E, H, K)) / np.sqrt(H) / u[None, :, None]]
    w3 = [pack_weight(m, "e2m1") for m in n((E, H, K)) / np.sqrt(H) / u[None, :, None]]
    return {
        "dyT": (n((N, T)) * s).astype(np.float32),
        "a1": n((H, E * C)).astype(np.float32),
        "a3": n((H, E * C)).astype(np.float32),
        "w2_words": np.stack([m[0] for m in w2]),
        "w2_scales": np.stack([m[1] for m in w2]),
        "w1_words": np.stack([m[0] for m in w1]),
        "w1_scales": np.stack([m[1] for m in w1]),
        "w3_words": np.stack([m[0] for m in w3]),
        "w3_scales": np.stack([m[1] for m in w3]),
        "gate": np.tile(np.random.uniform(0.2, 1.0, E * C), (N, 1)).astype(np.float32),
        "offs": striped(np.random.permutation(T)[:E * C]),
    }


def reference(dyT, a1, a3, w2_words, w2_scales, w1_words, w1_scales, w3_words, w3_scales, gate, offs):
    idx = unstriped(offs)
    w2 = np.stack([unpack_weight(w2_words[e], w2_scales[e], "e2m1") for e in range(E)])
    w1 = np.stack([unpack_weight(w1_words[e], w1_scales[e], "e2m1") for e in range(E)])
    w3 = np.stack([unpack_weight(w3_words[e], w3_scales[e], "e2m1") for e in range(E)])
    gq = mxq(f64(gate) * f64(dyT)[:, idx], 0, "e4m3")
    dh = by_expert(w2, gq)
    da1 = dh * f64(a3) * d_relu(f64(a1))
    da3 = dh * relu(f64(a1))
    dx = by_expert(w1, mxq(da1, 0, "e4m3")) + by_expert(w3, mxq(da3, 0, "e4m3"))
    out = np.zeros((K, T))
    out[:, idx] = dx
    return out

@@ -1,0 +1,209 @@
+from contextlib import ExitStack
+
+import concourse.mybir as mybir
+from concourse.masks import make_identity
+
+K, T, E, C, H, N = 128, 2048, 12, 128, 512, 512
+S = E * C
+P = 128
+PACK = 4
+PAIR = 2 * C
+PAIRS = S // PAIR
+FLOPS = 1207959552
+
+F32 = mybir.dt.float32
+BF16 = mybir.dt.bfloat16
+U32 = mybir.dt.uint32
+I32 = mybir.dt.int32
+U16 = mybir.dt.uint16
+U8 = mybir.dt.uint8
+FP8 = mybir.dt.float8_e4m3fn_x4
+FP4 = mybir.dt.float4_e2m1fn_x4
+MULT = mybir.AluOpType.mult
+ACT = mybir.ActivationFunctionType
+
+SAVED_CHUNKS = (256, 256, 512, 512)
+GATE_CHUNK = 512
+W2_GROUP = 4
+
+
+def tile_moe_bdx_glu_relu_kernel(
+    tc, dyT, a1, a3, w2_words, w2_scales, w1_words, w1_scales, w3_words, w3_scales, gate, offs, out
+):
+    nc = tc.nc
+    with ExitStack() as ctx:
+        held = ctx.enter_context(tc.tile_pool(name="held", bufs=1))
+        ring = ctx.enter_context(tc.tile_pool(name="ring", bufs=3))
+        psum_h = ctx.enter_context(tc.psum_pool(name="psum_h", bufs=2))
+        psum_t = ctx.enter_context(tc.psum_pool(name="psum_t", bufs=4))
+        psum_o = ctx.enter_context(tc.psum_pool(name="psum_o", bufs=2))
+
+        offsets = held.tile([P, S // 16], U16, name="offsets")
+        nc.sync.dma_start(offsets[:], offs)
+
+        w2_s = held.tile([P, E, H], U8, name="w2_s", align_bytes=64)
+        w1_s = held.tile([P, E, K], U8, name="w1_s", align_bytes=64)
+        w3_s = held.tile([P, E, K], U8, name="w3_s", align_bytes=64)
+        window = held.tile([P, T], F32, name="window", align_bytes=64)
+        for plane in (w2_s, w1_s, w3_s):
+            nc.vector.memset(plane[:].rearrange("p e n -> p (e n)").bitcast(I32), 0)
+        nc.vector.memset(window[:], 0.0)
+        ident = held.tile([P, P], F32, name="ident")
+        make_identity(nc, ident[:])
+
+        dy_rows = dyT.rearrange("(p d) t -> d p t", d=PACK)
+        dy = [held.tile([P, T], F32, name="dy%d" % d, align_bytes=64) for d in range(PACK)]
+        gates = [held.tile([P, GATE_CHUNK], F32, name="gate%d" % c, align_bytes=64) for c in range(S // GATE_CHUNK)]
+        w2_w = [held.tile([P, W2_GROUP, 2 * H], U8, name="w2_w%d" % q, align_bytes=64) for q in range(E // W2_GROUP)]
+        w1_w = held.tile([P, E, 2 * K], U8, name="w1_w", align_bytes=64)
+        w3_w = held.tile([P, E, 2 * K], U8, name="w3_w", align_bytes=64)
+        saved = [held.tile([P, 2, PACK, w], F32, name="saved%d" % c, align_bytes=64) for c, w in enumerate(SAVED_CHUNKS)]
+
+        def load_scales(tile, src):
+            rows = src.bitcast(I32)
+            for quad in range(4):
+                nc.sync.dma_start(
+                    tile[32 * quad : 32 * quad + 4, :, :].bitcast(I32),
+                    rows[:, :, 4 * quad : 4 * quad + 4, :].rearrange("e s f n -> f (e s) n"),
+                )
+
+        def load_words(tile, src):
+            nc.sync.dma_start(tile[:].bitcast(I32), src.bitcast(I32).rearrange("e s p n -> p (e s) n"))
+
+        def load_saved(c):
+            lo = sum(SAVED_CHUNKS[:c])
+            hi = lo + SAVED_CHUNKS[c]
+            for which, src in ((1, a1), (0, a3)):
+                nc.sync.dma_start(saved[c][:, which], src.rearrange("(p t) s -> p t s", t=PACK)[:, :, lo:hi])
+
+        nc.sync.dma_start(dy[0][:], dy_rows[0])
+        for c in range(S // GATE_CHUNK):
+            nc.sync.dma_start(gates[c][:], gate[0:P, c * GATE_CHUNK : (c + 1) * GATE_CHUNK])
+        nc.sync.dma_start(dy[1][:], dy_rows[1])
+        nc.sync.dma_start(dy[2][:], dy_rows[2])
+        nc.sync.dma_start(dy[3][:], dy_rows[3])
+        load_scales(w2_s, w2_scales)
+        load_words(w2_w[0], w2_words[0:W2_GROUP])
+        load_saved(0)
+        load_scales(w1_s, w1_scales)
+        load_scales(w3_s, w3_scales)
+        load_words(w1_w, w1_words)
+        load_words(w3_w, w3_words)
+        load_words(w2_w[1], w2_words[W2_GROUP : 2 * W2_GROUP])
+        load_saved(1)
+        load_saved(2)
+        load_words(w2_w[2], w2_words[2 * W2_GROUP : 3 * W2_GROUP])
+        load_saved(3)
+
+        g = held.tile([P, PACK, S], F32, name="g", align_bytes=64)
+
+        def gather(d, lo, hi):
+            c = lo // GATE_CHUNK
+            nc.vector.tensor_tensor(
+                g[:, d, lo:hi],
+                dy[d][:].indirect(offsets[:, lo // 16 : hi // 16]),
+                gates[c][:, lo - c * GATE_CHUNK : hi - c * GATE_CHUNK],
+                MULT,
+            )
+
+        for d in range(PACK - 1):
+            for c in range(S // GATE_CHUNK):
+                gather(d, c * GATE_CHUNK, (c + 1) * GATE_CHUNK)
+
+        g_il, g_codes, g_scales, dh_t = {}, {}, {}, {}
+        positive, da, da_codes, da_scales, dx = {}, {}, {}, {}, {}
+
+        def saved_of(k):
+            lo = k * PAIR
+            c = 0
+            while lo >= SAVED_CHUNKS[c]:
+                lo -= SAVED_CHUNKS[c]
+                c += 1
+            return saved[c], lo
+
+        def stage_gather(k):
+            gather(PACK - 1, k * PAIR, (k + 1) * PAIR)
+            g_il[k] = ring.tile([P, PAIR, PACK], BF16, name="g_il", align_bytes=64)
+            nc.scalar.copy(g_il[k][:], g[:, :, k * PAIR : (k + 1) * PAIR].rearrange("p d s -> p s d"))
+
+        def stage_first(k):
+            g_codes[k] = ring.tile([P, PAIR], U32, name="g_codes", align_bytes=64)
+            g_scales[k] = ring.tile([P, PAIR], U8, name="g_scales", align_bytes=64)
+            nc.vector.quantize_mx(out=g_codes[k][:].bitcast(FP8), scales=g_scales[k][:], in_=g_il[k][:].rearrange("p s d -> p (s d)"))
+            for j in range(2):
+                e = 2 * k + j
+                cols = slice(j * C, (j + 1) * C)
+                dh = psum_h.tile([P, H], F32, name="dh")
+                nc.tensor.matmul_mx(
+                    out=dh[:],
+                    lhsT=g_codes[k][:, cols].bitcast(FP8),
+                    lhsT_scale=g_scales[k][:, cols],
+                    rhs=w2_w[e // W2_GROUP][:, e % W2_GROUP, :].bitcast(FP4),
+                    rhs_scale=w2_s[:, e, :],
+                    start=True,
+                    stop=True,
+                )
+                dh_sb = ring.tile([P, PACK, P], F32, name="dh_sb", align_bytes=64)
+                nc.scalar.copy(dh_sb[:], dh[:].rearrange("p (m t) -> p t m", t=PACK))
+                dh_t[e] = psum_t.tile([P, PACK, C], F32, name="dh_t")
+                for t in range(PACK):
+                    nc.tensor.transpose(dh_t[e][:, t, :], dh_sb[:, t, :], ident[:])
+
+        def stage_saved(k):
+            tile, lo = saved_of(k)
+            relu = tile[:, 1, :, lo : lo + PAIR]
+            nc.scalar.activation(relu, relu, ACT.Relu)
+            positive[k] = ring.tile([P, PAIR, PACK], BF16, name="positive", align_bytes=64)
+            nc.scalar.activation(positive[k][:], relu.rearrange("p t s -> p s t"), ACT.Sign)
+
+        def stage_products(k):
+            tile, lo = saved_of(k)
+            da[k] = ring.tile([P, 2, 2, C, PACK], BF16, name="da", align_bytes=64)
+            for j in range(2):
+                e = 2 * k + j
+                nc.vector.tensor_tensor(
+                    da[k][:, j],
+                    dh_t[e][:].rearrange("p t c -> p c t").unsqueeze(1).to_broadcast([P, 2, C, PACK]),
+                    tile[:, :, :, lo + j * C : lo + (j + 1) * C].rearrange("p w t c -> p w c t"),
+                    MULT,
+                )
+
+        def stage_second(k):
+            da1 = da[k][:, :, 0].rearrange("p j c t -> p j (c t)")
+            nc.vector.tensor_tensor(da1, da1, positive[k][:].rearrange("p (j c) t -> p j (c t)", j=2), MULT)
+            da_codes[k] = ring.tile([P, 2, 2, C], U32, name="da_codes", align_bytes=64)
+            da_scales[k] = ring.tile([P, 2, 2, C], U8, name="da_scales", align_bytes=64)
+            nc.vector.quantize_mx(
+                out=da_codes[k][:].rearrange("p j w c -> p (j w c)").bitcast(FP8),
+                scales=da_scales[k][:].rearrange("p j w c -> p (j w c)"),
+                in_=da[k][:].rearrange("p j w c t -> p (j w c t)"),
+            )
+            acc = psum_o.tile([P, PAIR], F32, name="acc")
+            for j in range(2):
+                e = 2 * k + j
+                for w, (words, scales) in enumerate(((w1_w, w1_s), (w3_w, w3_s))):
+                    nc.tensor.matmul_mx(
+                        out=acc[:, j * C : (j + 1) * C],
+                        lhsT=words[:, e, :].bitcast(FP4),
+                        lhsT_scale=scales[:, e, :],
+                        rhs=da_codes[k][:, j, w, :].bitcast(FP8),
+                        rhs_scale=da_scales[k][:, j, w, :],
+                        start=(w == 0),
+                        stop=(w == 1),
+                    )
+            dx[k] = ring.tile([P, PAIR], F32, name="dx", align_bytes=64)
+            nc.scalar.copy(dx[k][:], acc[:])
+
+        def stage_scatter(k):
+            nc.vector.tensor_copy(window[:].indirect(offsets[:, k * PAIR // 16 : (k + 1) * PAIR // 16]), dx[k][:])
+
+        stages = (stage_gather, stage_first, stage_products, stage_second, stage_scatter)
+        for step in range(PAIRS + len(stages) - 1):
+            if step < PAIRS:
+                stage_saved(step)
+            for lag in range(len(stages) - 1, -1, -1):
+                k = step - lag
+                if 0 <= k < PAIRS:
+                    stages[lag](k)
+
+        nc.sync.dma_start(out, window[:])

@@ -80,9 +80,9 @@ def tile_moe_bdx_glu_relu_kernel(
         for c in range(S // GATE_CHUNK):
             nc.sync.dma_start(gates[c][:], gate[0:P, c * GATE_CHUNK : (c + 1) * GATE_CHUNK])
         nc.sync.dma_start(dy[1][:], dy_rows[1])
+        load_scales(w2_s, w2_scales)
         nc.sync.dma_start(dy[2][:], dy_rows[2])
         nc.sync.dma_start(dy[3][:], dy_rows[3])
-        load_scales(w2_s, w2_scales)
         load_words(w2_w[0], w2_words[0:W2_GROUP])
         load_saved(0)
         load_scales(w1_s, w1_scales)
@@ -124,7 +124,10 @@ def tile_moe_bdx_glu_relu_kernel(
         def stage_gather(k):
             gather(PACK - 1, k * PAIR, (k + 1) * PAIR)
             g_il[k] = ring.tile([P, PAIR, PACK], BF16, name="g_il", align_bytes=64)
-            nc.scalar.copy(g_il[k][:], g[:, :, k * PAIR : (k + 1) * PAIR].rearrange("p d s -> p s d"))
+            nc.scalar.copy(
+                g_il[k][:].rearrange("p (q i) d -> p q d i", i=4),
+                g[:, :, k * PAIR : (k + 1) * PAIR].rearrange("p d (q i) -> p q d i", i=4),
+            )
 
         def stage_first(k):
             g_codes[k] = ring.tile([P, PAIR], U32, name="g_codes", align_bytes=64)
@@ -154,23 +157,30 @@ def tile_moe_bdx_glu_relu_kernel(
             relu = tile[:, 1, :, lo : lo + PAIR]
             nc.scalar.activation(relu, relu, ACT.Relu)
             positive[k] = ring.tile([P, PAIR, PACK], BF16, name="positive", align_bytes=64)
-            nc.scalar.activation(positive[k][:], relu.rearrange("p t s -> p s t"), ACT.Sign)
+            nc.scalar.activation(
+                positive[k][:].rearrange("p (q i) t -> p q t i", i=4),
+                relu.rearrange("p t (q i) -> p q t i", i=4),
+                ACT.Sign,
+            )
 
         def stage_products(k):
             tile, lo = saved_of(k)
             da[k] = ring.tile([P, 2, 2, C, PACK], BF16, name="da", align_bytes=64)
             for j in range(2):
                 e = 2 * k + j
-                nc.vector.tensor_tensor(
-                    da[k][:, j],
-                    dh_t[e][:].rearrange("p t c -> p c t").unsqueeze(1).to_broadcast([P, 2, C, PACK]),
-                    tile[:, :, :, lo + j * C : lo + (j + 1) * C].rearrange("p w t c -> p w c t"),
-                    MULT,
-                )
+                for w in range(2):
+                    nc.vector.tensor_tensor(
+                        da[k][:, j, w].rearrange("p (q i) t -> p q t i", i=4),
+                        dh_t[e][:].rearrange("p t (q i) -> p q t i", i=4),
+                        tile[:, w, :, lo + j * C : lo + (j + 1) * C].rearrange("p t (q i) -> p q t i", i=4),
+                        MULT,
+                    )
 
-        def stage_second(k):
+        def stage_mask(k):
             da1 = da[k][:, :, 0].rearrange("p j c t -> p j (c t)")
             nc.vector.tensor_tensor(da1, da1, positive[k][:].rearrange("p (j c) t -> p j (c t)", j=2), MULT)
+
+        def stage_second(k):
             da_codes[k] = ring.tile([P, 2, 2, C], U32, name="da_codes", align_bytes=64)
             da_scales[k] = ring.tile([P, 2, 2, C], U8, name="da_scales", align_bytes=64)
             nc.vector.quantize_mx(
@@ -197,13 +207,18 @@ def tile_moe_bdx_glu_relu_kernel(
         def stage_scatter(k):
             nc.vector.tensor_copy(window[:].indirect(offsets[:, k * PAIR // 16 : (k + 1) * PAIR // 16]), dx[k][:])
 
-        stages = (stage_gather, stage_first, stage_products, stage_second, stage_scatter)
-        for step in range(PAIRS + len(stages) - 1):
-            if step < PAIRS:
-                stage_saved(step)
-            for lag in range(len(stages) - 1, -1, -1):
-                k = step - lag
-                if 0 <= k < PAIRS:
-                    stages[lag](k)
+        stages = (
+            (stage_gather, 0),
+            (stage_saved, 1),
+            (stage_first, 1),
+            (stage_mask, 3),
+            (stage_products, 2),
+            (stage_second, 3),
+            (stage_scatter, 4),
+        )
+        for step in range(PAIRS + 4):
+            for stage, lag in stages:
+                if 0 <= step - lag < PAIRS:
+                    stage(step - lag)
 
         nc.sync.dma_start(out, window[:])

@@ -24,7 +24,8 @@ ACT = mybir.ActivationFunctionType
 
 SAVED_CHUNKS = (256, 256, 512, 512)
 GATE_CHUNK = 512
-W2_GROUP = 4
+GATED_BY_VECTOR = 1024
+W2_GROUPS = (2, 2, 4, 4)
 
 
 def tile_moe_bdx_glu_relu_kernel(
@@ -54,7 +55,7 @@ def tile_moe_bdx_glu_relu_kernel(
         dy_rows = dyT.rearrange("(p d) t -> d p t", d=PACK)
         dy = [held.tile([P, T], F32, name="dy%d" % d, align_bytes=64) for d in range(PACK)]
         gates = [held.tile([P, GATE_CHUNK], F32, name="gate%d" % c, align_bytes=64) for c in range(S // GATE_CHUNK)]
-        w2_w = [held.tile([P, W2_GROUP, 2 * H], U8, name="w2_w%d" % q, align_bytes=64) for q in range(E // W2_GROUP)]
+        w2_w = [held.tile([P, n, 2 * H], U8, name="w2_w%d" % q, align_bytes=64) for q, n in enumerate(W2_GROUPS)]
         w1_w = held.tile([P, E, 2 * K], U8, name="w1_w", align_bytes=64)
         w3_w = held.tile([P, E, 2 * K], U8, name="w3_w", align_bytes=64)
         saved = [held.tile([P, 2, PACK, w], F32, name="saved%d" % c, align_bytes=64) for c, w in enumerate(SAVED_CHUNKS)]
@@ -62,7 +63,7 @@ def tile_moe_bdx_glu_relu_kernel(
         def load_scales(tile, src):
             rows = src.bitcast(I32)
             for quad in range(4):
-                nc.sync.dma_start(
+                nc.gpsimd.dma_start(
                     tile[32 * quad : 32 * quad + 4, :, :].bitcast(I32),
                     rows[:, :, 4 * quad : 4 * quad + 4, :].rearrange("e s f n -> f (e s) n"),
                 )
@@ -76,39 +77,52 @@ def tile_moe_bdx_glu_relu_kernel(
             for which, src in ((1, a1), (0, a3)):
                 nc.sync.dma_start(saved[c][:, which], src.rearrange("(p t) s -> p t s", t=PACK)[:, :, lo:hi])
 
+        def load_w2(q):
+            first = sum(W2_GROUPS[:q])
+            load_words(w2_w[q], w2_words[first : first + W2_GROUPS[q]])
+
         nc.sync.dma_start(dy[0][:], dy_rows[0])
-        for c in range(S // GATE_CHUNK):
+        def load_gate(c):
             nc.sync.dma_start(gates[c][:], gate[0:P, c * GATE_CHUNK : (c + 1) * GATE_CHUNK])
-        nc.sync.dma_start(dy[1][:], dy_rows[1])
+
         load_scales(w2_s, w2_scales)
-        nc.sync.dma_start(dy[2][:], dy_rows[2])
-        nc.sync.dma_start(dy[3][:], dy_rows[3])
-        load_words(w2_w[0], w2_words[0:W2_GROUP])
-        load_saved(0)
         load_scales(w1_s, w1_scales)
         load_scales(w3_s, w3_scales)
+        load_gate(0)
+        load_gate(1)
+        nc.sync.dma_start(dy[1][:], dy_rows[1])
+        nc.sync.dma_start(dy[2][:], dy_rows[2])
+        nc.sync.dma_start(dy[3][:], dy_rows[3])
+        load_w2(0)
+        load_saved(0)
+        load_w2(1)
         load_words(w1_w, w1_words)
         load_words(w3_w, w3_words)
-        load_words(w2_w[1], w2_words[W2_GROUP : 2 * W2_GROUP])
+        load_gate(2)
         load_saved(1)
+        load_w2(2)
         load_saved(2)
-        load_words(w2_w[2], w2_words[2 * W2_GROUP : 3 * W2_GROUP])
+        load_w2(3)
         load_saved(3)
+
+        w2_of = [(w2_w[q], i) for q, n in enumerate(W2_GROUPS) for i in range(n)]
 
         g = held.tile([P, PACK, S], F32, name="g", align_bytes=64)
 
         def gather(d, lo, hi):
-            c = lo // GATE_CHUNK
-            nc.vector.tensor_tensor(
-                g[:, d, lo:hi],
-                dy[d][:].indirect(offsets[:, lo // 16 : hi // 16]),
-                gates[c][:, lo - c * GATE_CHUNK : hi - c * GATE_CHUNK],
-                MULT,
-            )
+            looked_up = dy[d][:].indirect(offsets[:, lo // 16 : hi // 16])
+            if lo < GATED_BY_VECTOR:
+                c = lo // GATE_CHUNK
+                nc.vector.tensor_tensor(
+                    g[:, d, lo:hi], looked_up, gates[c][:, lo - c * GATE_CHUNK : hi - c * GATE_CHUNK], MULT
+                )
+            else:
+                nc.vector.tensor_copy(g[:, d, lo:hi], looked_up)
 
         for d in range(PACK - 1):
             for c in range(S // GATE_CHUNK):
-                gather(d, c * GATE_CHUNK, (c + 1) * GATE_CHUNK)
+                if (d, c) != (2, 2):
+                    gather(d, c * GATE_CHUNK, (c + 1) * GATE_CHUNK)
 
         g_il, g_codes, g_scales, dh_t = {}, {}, {}, {}
         positive, da, da_codes, da_scales, dx = {}, {}, {}, {}, {}
@@ -122,8 +136,19 @@ def tile_moe_bdx_glu_relu_kernel(
             return saved[c], lo
 
         def stage_gather(k):
+            if k == 2:
+                gather(2, 2 * GATE_CHUNK, 3 * GATE_CHUNK)
             gather(PACK - 1, k * PAIR, (k + 1) * PAIR)
             g_il[k] = ring.tile([P, PAIR, PACK], BF16, name="g_il", align_bytes=64)
+            if k * PAIR >= GATED_BY_VECTOR:
+                lo = k * PAIR % GATE_CHUNK
+                nc.gpsimd.tensor_tensor(
+                    g_il[k][:],
+                    g[:, :, k * PAIR : (k + 1) * PAIR].rearrange("p d s -> p s d"),
+                    gates[k * PAIR // GATE_CHUNK][:, lo : lo + PAIR].unsqueeze(2).to_broadcast([P, PAIR, PACK]),
+                    MULT,
+                )
+                return
             nc.scalar.copy(
                 g_il[k][:].rearrange("p (q i) d -> p q d i", i=4),
                 g[:, :, k * PAIR : (k + 1) * PAIR].rearrange("p d (q i) -> p q d i", i=4),
@@ -141,7 +166,7 @@ def tile_moe_bdx_glu_relu_kernel(
                     out=dh[:],
                     lhsT=g_codes[k][:, cols].bitcast(FP8),
                     lhsT_scale=g_scales[k][:, cols],
-                    rhs=w2_w[e // W2_GROUP][:, e % W2_GROUP, :].bitcast(FP4),
+                    rhs=w2_of[e][0][:, w2_of[e][1], :].bitcast(FP4),
                     rhs_scale=w2_s[:, e, :],
                     start=True,
                     stop=True,
@@ -169,9 +194,14 @@ def tile_moe_bdx_glu_relu_kernel(
             for j in range(2):
                 e = 2 * k + j
                 for w in range(2):
-                    nc.vector.tensor_tensor(
+                    engine, src = nc.vector, dh_t[e]
+                    if w == 1 and j == 1 and 2 <= k <= 4:
+                        engine = nc.gpsimd
+                        src = ring.tile([P, PACK, C], F32, name="dh_g", align_bytes=64)
+                        nc.scalar.copy(src[:], dh_t[e][:])
+                    engine.tensor_tensor(
                         da[k][:, j, w].rearrange("p (q i) t -> p q t i", i=4),
-                        dh_t[e][:].rearrange("p t (q i) -> p q t i", i=4),
+                        src[:].rearrange("p t (q i) -> p q t i", i=4),
                         tile[:, w, :, lo + j * C : lo + (j + 1) * C].rearrange("p t (q i) -> p q t i", i=4),
                         MULT,
                     )
@@ -209,10 +239,10 @@ def tile_moe_bdx_glu_relu_kernel(
 
         stages = (
             (stage_gather, 0),
-            (stage_saved, 1),
             (stage_first, 1),
-            (stage_mask, 3),
             (stage_products, 2),
+            (stage_saved, 1),
+            (stage_mask, 3),
             (stage_second, 3),
             (stage_scatter, 4),
         )

@@ -3,13 +3,16 @@ from contextlib import ExitStack
 import concourse.mybir as mybir
 from concourse.masks import make_identity
 
-K, T, E, C, H, N = 128, 2048, 12, 128, 512, 512
-S = E * C
+K, T, E, C, H = 128, 2048, 12, 128, 512
+SLOTS = E * C
 P = 128
 PACK = 4
+RUN = 4
 PAIR = 2 * C
-PAIRS = S // PAIR
-FLOPS = 1207959552
+PAIRS = SLOTS // PAIR
+OFFSETS_PER_COLUMN = 16
+
+FLOPS = 2 * SLOTS * H * (H + 2 * K)
 
 F32 = mybir.dt.float32
 BF16 = mybir.dt.bfloat16
@@ -17,15 +20,18 @@ U32 = mybir.dt.uint32
 I32 = mybir.dt.int32
 U16 = mybir.dt.uint16
 U8 = mybir.dt.uint8
-FP8 = mybir.dt.float8_e4m3fn_x4
-FP4 = mybir.dt.float4_e2m1fn_x4
+FP8X4 = mybir.dt.float8_e4m3fn_x4
+FP4X4 = mybir.dt.float4_e2m1fn_x4
 MULT = mybir.AluOpType.mult
 ACT = mybir.ActivationFunctionType
 
-SAVED_CHUNKS = (256, 256, 512, 512)
-GATE_CHUNK = 512
-GATED_BY_VECTOR = 1024
-W2_GROUPS = (2, 2, 4, 4)
+GROUPS = ((0, 512), (512, SLOTS))
+
+SAVED_WIDTHS = (256, 256, 256, 256, 512)
+
+W2_COUNTS = (2, 2, 4, 4)
+
+GPSIMD_DA3_EXPERTS = (7, 9)
 
 
 def tile_moe_bdx_glu_relu_kernel(
@@ -35,215 +41,229 @@ def tile_moe_bdx_glu_relu_kernel(
     with ExitStack() as ctx:
         held = ctx.enter_context(tc.tile_pool(name="held", bufs=1))
         ring = ctx.enter_context(tc.tile_pool(name="ring", bufs=3))
-        psum_h = ctx.enter_context(tc.psum_pool(name="psum_h", bufs=2))
-        psum_t = ctx.enter_context(tc.psum_pool(name="psum_t", bufs=4))
-        psum_o = ctx.enter_context(tc.psum_pool(name="psum_o", bufs=2))
+        psum_dh = ctx.enter_context(tc.psum_pool(name="psum_dh", bufs=2))
+        psum_turned = ctx.enter_context(tc.psum_pool(name="psum_turned", bufs=4))
+        psum_dx = ctx.enter_context(tc.psum_pool(name="psum_dx", bufs=2))
 
-        offsets = held.tile([P, S // 16], U16, name="offsets")
+        offsets = held.tile([P, SLOTS // OFFSETS_PER_COLUMN], U16, name="offsets")
         nc.sync.dma_start(offsets[:], offs)
 
         w2_s = held.tile([P, E, H], U8, name="w2_s", align_bytes=64)
         w1_s = held.tile([P, E, K], U8, name="w1_s", align_bytes=64)
         w3_s = held.tile([P, E, K], U8, name="w3_s", align_bytes=64)
         window = held.tile([P, T], F32, name="window", align_bytes=64)
-        for plane in (w2_s, w1_s, w3_s):
-            nc.vector.memset(plane[:].rearrange("p e n -> p (e n)").bitcast(I32), 0)
+        for scale_tile in (w2_s, w1_s, w3_s):
+            nc.vector.memset(scale_tile[:].rearrange("p e n -> p (e n)").bitcast(I32), 0)
         nc.vector.memset(window[:], 0.0)
-        ident = held.tile([P, P], F32, name="ident")
-        make_identity(nc, ident[:])
+        identity = held.tile([P, P], F32, name="identity")
+        make_identity(nc, identity[:])
 
         dy_rows = dyT.rearrange("(p d) t -> d p t", d=PACK)
         dy = [held.tile([P, T], F32, name="dy%d" % d, align_bytes=64) for d in range(PACK)]
-        gates = [held.tile([P, GATE_CHUNK], F32, name="gate%d" % c, align_bytes=64) for c in range(S // GATE_CHUNK)]
-        w2_w = [held.tile([P, n, 2 * H], U8, name="w2_w%d" % q, align_bytes=64) for q, n in enumerate(W2_GROUPS)]
+        gates = [held.tile([P, hi - lo], F32, name="gate%d" % lo, align_bytes=64) for lo, hi in GROUPS]
+        w2_w = [held.tile([P, n, 2 * H], U8, name="w2_w%d" % q, align_bytes=64) for q, n in enumerate(W2_COUNTS)]
         w1_w = held.tile([P, E, 2 * K], U8, name="w1_w", align_bytes=64)
         w3_w = held.tile([P, E, 2 * K], U8, name="w3_w", align_bytes=64)
-        saved = [held.tile([P, 2, PACK, w], F32, name="saved%d" % c, align_bytes=64) for c, w in enumerate(SAVED_CHUNKS)]
+        a1_in = [held.tile([P, PACK, n], F32, name="a1_in%d" % c, align_bytes=64) for c, n in enumerate(SAVED_WIDTHS)]
+        a3_in = [held.tile([P, PACK, n], F32, name="a3_in%d" % c, align_bytes=64) for c, n in enumerate(SAVED_WIDTHS)]
 
-        def load_scales(tile, src):
-            rows = src.bitcast(I32)
+        def load_scales(tile, source):
+            rows = source.bitcast(I32)
             for quad in range(4):
-                nc.gpsimd.dma_start(
+                nc.sync.dma_start(
                     tile[32 * quad : 32 * quad + 4, :, :].bitcast(I32),
                     rows[:, :, 4 * quad : 4 * quad + 4, :].rearrange("e s f n -> f (e s) n"),
                 )
 
-        def load_words(tile, src):
-            nc.sync.dma_start(tile[:].bitcast(I32), src.bitcast(I32).rearrange("e s p n -> p (e s) n"))
-
-        def load_saved(c):
-            lo = sum(SAVED_CHUNKS[:c])
-            hi = lo + SAVED_CHUNKS[c]
-            for which, src in ((1, a1), (0, a3)):
-                nc.sync.dma_start(saved[c][:, which], src.rearrange("(p t) s -> p t s", t=PACK)[:, :, lo:hi])
+        def load_words(tile, source):
+            nc.sync.dma_start(tile[:].bitcast(I32), source.bitcast(I32).rearrange("e s p n -> p (e s) n"))
 
         def load_w2(q):
-            first = sum(W2_GROUPS[:q])
-            load_words(w2_w[q], w2_words[first : first + W2_GROUPS[q]])
+            first = sum(W2_COUNTS[:q])
+            load_words(w2_w[q], w2_words[first : first + W2_COUNTS[q]])
+
+        def load_saved(c):
+            lo = sum(SAVED_WIDTHS[:c])
+            for tile, source in ((a1_in[c], a1), (a3_in[c], a3)):
+                rows = source.rearrange("(p t) s -> p t s", t=PACK)
+                nc.sync.dma_start(tile[:], rows[:, :, lo : lo + SAVED_WIDTHS[c]])
+
+        def load_gate(group):
+            lo, hi = GROUPS[group]
+            nc.sync.dma_start(gates[group][:], gate[0:P, lo:hi])
 
         nc.sync.dma_start(dy[0][:], dy_rows[0])
-        def load_gate(c):
-            nc.sync.dma_start(gates[c][:], gate[0:P, c * GATE_CHUNK : (c + 1) * GATE_CHUNK])
-
-        load_scales(w2_s, w2_scales)
-        load_scales(w1_s, w1_scales)
-        load_scales(w3_s, w3_scales)
         load_gate(0)
-        load_gate(1)
-        nc.sync.dma_start(dy[1][:], dy_rows[1])
-        nc.sync.dma_start(dy[2][:], dy_rows[2])
-        nc.sync.dma_start(dy[3][:], dy_rows[3])
+        for d in range(1, PACK):
+            nc.sync.dma_start(dy[d][:], dy_rows[d])
+        load_scales(w2_s, w2_scales)
         load_w2(0)
         load_saved(0)
+        load_gate(1)
         load_w2(1)
+        load_scales(w1_s, w1_scales)
+        load_scales(w3_s, w3_scales)
         load_words(w1_w, w1_words)
         load_words(w3_w, w3_words)
-        load_gate(2)
         load_saved(1)
         load_w2(2)
         load_saved(2)
-        load_w2(3)
         load_saved(3)
+        load_w2(3)
+        load_saved(4)
 
-        w2_of = [(w2_w[q], i) for q, n in enumerate(W2_GROUPS) for i in range(n)]
+        w2_of = [w2_w[q][:, i, :] for q, n in enumerate(W2_COUNTS) for i in range(n)]
 
-        g = held.tile([P, PACK, S], F32, name="g", align_bytes=64)
+        gathered = [held.tile([P, PACK, hi - lo], F32, name="gathered%d" % lo, align_bytes=64) for lo, hi in GROUPS]
+
+        def offsets_of(lo, hi):
+            return offsets[:, lo // OFFSETS_PER_COLUMN : hi // OFFSETS_PER_COLUMN]
 
         def gather(d, lo, hi):
-            looked_up = dy[d][:].indirect(offsets[:, lo // 16 : hi // 16])
-            if lo < GATED_BY_VECTOR:
-                c = lo // GATE_CHUNK
-                nc.vector.tensor_tensor(
-                    g[:, d, lo:hi], looked_up, gates[c][:, lo - c * GATE_CHUNK : hi - c * GATE_CHUNK], MULT
-                )
+            looked_up = dy[d][:].indirect(offsets_of(lo, hi))
+            if hi <= GROUPS[0][1]:
+                nc.vector.tensor_tensor(gathered[0][:, d, lo:hi], looked_up, gates[0][:, lo:hi], MULT)
             else:
-                nc.vector.tensor_copy(g[:, d, lo:hi], looked_up)
+                first = GROUPS[1][0]
+                nc.vector.tensor_copy(gathered[1][:, d, lo - first : hi - first], looked_up)
 
-        for d in range(PACK - 1):
-            for c in range(S // GATE_CHUNK):
-                if (d, c) != (2, 2):
-                    gather(d, c * GATE_CHUNK, (c + 1) * GATE_CHUNK)
+        def runs(block):
+            return block.rearrange("p t (q i) -> p q t i", i=RUN)
 
-        g_il, g_codes, g_scales, dh_t = {}, {}, {}, {}
-        positive, da, da_codes, da_scales, dx = {}, {}, {}, {}, {}
+        def runs_out(block):
+            return block.rearrange("p (q i) t -> p q t i", i=RUN)
 
-        def saved_of(k):
-            lo = k * PAIR
+        def one_by_one(block):
+            return block.rearrange("p t c -> p c t")
+
+        g, g_codes, g_scales, turned = {}, {}, {}, {}
+        relu, positive, da, da_codes, da_scales, dx = {}, {}, {}, {}, {}, {}
+
+        def saved_of(tiles, pair):
+            lo = pair * PAIR
             c = 0
-            while lo >= SAVED_CHUNKS[c]:
-                lo -= SAVED_CHUNKS[c]
+            while lo >= SAVED_WIDTHS[c]:
+                lo -= SAVED_WIDTHS[c]
                 c += 1
-            return saved[c], lo
+            return tiles[c][:, :, lo : lo + PAIR]
 
-        def stage_gather(k):
-            if k == 2:
-                gather(2, 2 * GATE_CHUNK, 3 * GATE_CHUNK)
-            gather(PACK - 1, k * PAIR, (k + 1) * PAIR)
-            g_il[k] = ring.tile([P, PAIR, PACK], BF16, name="g_il", align_bytes=64)
-            if k * PAIR >= GATED_BY_VECTOR:
-                lo = k * PAIR % GATE_CHUNK
+        def stage_gather(pair):
+            lo = pair * PAIR
+            group = int(lo >= GROUPS[1][0])
+            if group == 0:
+                gather(3, lo, lo + PAIR)
+            elif pair % 2 == 0:
+                gather(2, lo, lo + 2 * PAIR)
+                gather(3, lo, lo + 2 * PAIR)
+            g[pair] = ring.tile([P, PAIR, PACK], BF16, name="g", align_bytes=64)
+            lo -= GROUPS[group][0]
+            if group == 0:
+                nc.scalar.copy(runs_out(g[pair][:]), runs(gathered[0][:, :, lo : lo + PAIR]))
+                return
+            for j in range(2):
+                cols = slice(lo + j * C, lo + (j + 1) * C)
                 nc.gpsimd.tensor_tensor(
-                    g_il[k][:],
-                    g[:, :, k * PAIR : (k + 1) * PAIR].rearrange("p d s -> p s d"),
-                    gates[k * PAIR // GATE_CHUNK][:, lo : lo + PAIR].unsqueeze(2).to_broadcast([P, PAIR, PACK]),
+                    g[pair][:, j * C : (j + 1) * C, :],
+                    one_by_one(gathered[1][:, :, cols]),
+                    gates[1][:, cols].unsqueeze(2).to_broadcast([P, C, PACK]),
                     MULT,
                 )
-                return
-            nc.scalar.copy(
-                g_il[k][:].rearrange("p (q i) d -> p q d i", i=4),
-                g[:, :, k * PAIR : (k + 1) * PAIR].rearrange("p d (q i) -> p q d i", i=4),
-            )
 
-        def stage_first(k):
-            g_codes[k] = ring.tile([P, PAIR], U32, name="g_codes", align_bytes=64)
-            g_scales[k] = ring.tile([P, PAIR], U8, name="g_scales", align_bytes=64)
-            nc.vector.quantize_mx(out=g_codes[k][:].bitcast(FP8), scales=g_scales[k][:], in_=g_il[k][:].rearrange("p s d -> p (s d)"))
+        def stage_first_product(pair):
+            g_codes[pair] = ring.tile([P, PAIR], U32, name="g_codes", align_bytes=64)
+            g_scales[pair] = ring.tile([P, PAIR], U8, name="g_scales", align_bytes=64)
+            nc.vector.quantize_mx(
+                out=g_codes[pair][:].bitcast(FP8X4),
+                scales=g_scales[pair][:],
+                in_=g[pair][:].rearrange("p s d -> p (s d)"),
+            )
             for j in range(2):
-                e = 2 * k + j
+                e = 2 * pair + j
                 cols = slice(j * C, (j + 1) * C)
-                dh = psum_h.tile([P, H], F32, name="dh")
+                dh = psum_dh.tile([P, H], F32, name="dh")
                 nc.tensor.matmul_mx(
                     out=dh[:],
-                    lhsT=g_codes[k][:, cols].bitcast(FP8),
-                    lhsT_scale=g_scales[k][:, cols],
-                    rhs=w2_of[e][0][:, w2_of[e][1], :].bitcast(FP4),
+                    lhsT=g_codes[pair][:, cols].bitcast(FP8X4),
+                    lhsT_scale=g_scales[pair][:, cols],
+                    rhs=w2_of[e].bitcast(FP4X4),
                     rhs_scale=w2_s[:, e, :],
                     start=True,
                     stop=True,
                 )
-                dh_sb = ring.tile([P, PACK, P], F32, name="dh_sb", align_bytes=64)
-                nc.scalar.copy(dh_sb[:], dh[:].rearrange("p (m t) -> p t m", t=PACK))
-                dh_t[e] = psum_t.tile([P, PACK, C], F32, name="dh_t")
+                dh_blocks = ring.tile([P, PACK, P], F32, name="dh_blocks", align_bytes=64)
+                nc.scalar.copy(dh_blocks[:], dh[:].rearrange("p (m t) -> p t m", t=PACK))
+                turned[e] = psum_turned.tile([P, PACK, C], F32, name="turned")
                 for t in range(PACK):
-                    nc.tensor.transpose(dh_t[e][:, t, :], dh_sb[:, t, :], ident[:])
+                    nc.tensor.transpose(turned[e][:, t, :], dh_blocks[:, t, :], identity[:])
 
-        def stage_saved(k):
-            tile, lo = saved_of(k)
-            relu = tile[:, 1, :, lo : lo + PAIR]
-            nc.scalar.activation(relu, relu, ACT.Relu)
-            positive[k] = ring.tile([P, PAIR, PACK], BF16, name="positive", align_bytes=64)
-            nc.scalar.activation(
-                positive[k][:].rearrange("p (q i) t -> p q t i", i=4),
-                relu.rearrange("p t (q i) -> p q t i", i=4),
-                ACT.Sign,
-            )
+        def stage_saved(pair):
+            relu[pair] = ring.tile([P, PACK, PAIR], F32, name="relu", align_bytes=64)
+            nc.scalar.activation(relu[pair][:], saved_of(a1_in, pair), ACT.Relu)
+            positive[pair] = ring.tile([P, PAIR, PACK], BF16, name="positive", align_bytes=64)
+            nc.scalar.activation(runs_out(positive[pair][:]), runs(relu[pair][:]), ACT.Sign)
 
-        def stage_products(k):
-            tile, lo = saved_of(k)
-            da[k] = ring.tile([P, 2, 2, C, PACK], BF16, name="da", align_bytes=64)
-            for j in range(2):
-                e = 2 * k + j
-                for w in range(2):
-                    engine, src = nc.vector, dh_t[e]
-                    if w == 1 and j == 1 and 2 <= k <= 4:
-                        engine = nc.gpsimd
-                        src = ring.tile([P, PACK, C], F32, name="dh_g", align_bytes=64)
-                        nc.scalar.copy(src[:], dh_t[e][:])
-                    engine.tensor_tensor(
-                        da[k][:, j, w].rearrange("p (q i) t -> p q t i", i=4),
-                        src[:].rearrange("p t (q i) -> p q t i", i=4),
-                        tile[:, w, :, lo + j * C : lo + (j + 1) * C].rearrange("p t (q i) -> p q t i", i=4),
-                        MULT,
-                    )
+        def stage_products(pair):
+            da[pair] = ring.tile([P, 2, 2, C, PACK], BF16, name="da", align_bytes=64)
+            for which, factor in enumerate((saved_of(a3_in, pair), relu[pair][:])):
+                for j in range(2):
+                    e = 2 * pair + j
+                    cols = slice(j * C, (j + 1) * C)
+                    if which == 1 and e in GPSIMD_DA3_EXPERTS:
+                        dh_copy = ring.tile([P, PACK, C], F32, name="dh_copy", align_bytes=64)
+                        nc.scalar.copy(dh_copy[:], turned[e][:])
+                        nc.gpsimd.tensor_tensor(
+                            da[pair][:, which, j], one_by_one(dh_copy[:]), one_by_one(factor[:, :, cols]), MULT
+                        )
+                    else:
+                        nc.vector.tensor_tensor(
+                            runs_out(da[pair][:, which, j]), runs(turned[e][:]), runs(factor[:, :, cols]), MULT
+                        )
 
-        def stage_mask(k):
-            da1 = da[k][:, :, 0].rearrange("p j c t -> p j (c t)")
-            nc.vector.tensor_tensor(da1, da1, positive[k][:].rearrange("p (j c) t -> p j (c t)", j=2), MULT)
+        def stage_mask(pair):
+            da1 = da[pair][:, 0].rearrange("p j c t -> p (j c t)")
+            nc.vector.tensor_tensor(da1, da1, positive[pair][:].rearrange("p c t -> p (c t)"), MULT)
 
-        def stage_second(k):
-            da_codes[k] = ring.tile([P, 2, 2, C], U32, name="da_codes", align_bytes=64)
-            da_scales[k] = ring.tile([P, 2, 2, C], U8, name="da_scales", align_bytes=64)
+        def stage_second_product(pair):
+            da_codes[pair] = ring.tile([P, 2, 2, C], U32, name="da_codes", align_bytes=64)
+            da_scales[pair] = ring.tile([P, 2, 2, C], U8, name="da_scales", align_bytes=64)
             nc.vector.quantize_mx(
-                out=da_codes[k][:].rearrange("p j w c -> p (j w c)").bitcast(FP8),
-                scales=da_scales[k][:].rearrange("p j w c -> p (j w c)"),
-                in_=da[k][:].rearrange("p j w c t -> p (j w c t)"),
+                out=da_codes[pair][:].rearrange("p w j c -> p (w j c)").bitcast(FP8X4),
+                scales=da_scales[pair][:].rearrange("p w j c -> p (w j c)"),
+                in_=da[pair][:].rearrange("p w j c t -> p (w j c t)"),
             )
-            acc = psum_o.tile([P, PAIR], F32, name="acc")
+            sums = psum_dx.tile([P, PAIR], F32, name="sums")
             for j in range(2):
-                e = 2 * k + j
-                for w, (words, scales) in enumerate(((w1_w, w1_s), (w3_w, w3_s))):
+                e = 2 * pair + j
+                for which, (words, scales) in enumerate(((w1_w, w1_s), (w3_w, w3_s))):
                     nc.tensor.matmul_mx(
-                        out=acc[:, j * C : (j + 1) * C],
-                        lhsT=words[:, e, :].bitcast(FP4),
+                        out=sums[:, j * C : (j + 1) * C],
+                        lhsT=words[:, e, :].bitcast(FP4X4),
                         lhsT_scale=scales[:, e, :],
-                        rhs=da_codes[k][:, j, w, :].bitcast(FP8),
-                        rhs_scale=da_scales[k][:, j, w, :],
-                        start=(w == 0),
-                        stop=(w == 1),
+                        rhs=da_codes[pair][:, which, j, :].bitcast(FP8X4),
+                        rhs_scale=da_scales[pair][:, which, j, :],
+                        start=(which == 0),
+                        stop=(which == 1),
                     )
-            dx[k] = ring.tile([P, PAIR], F32, name="dx", align_bytes=64)
-            nc.scalar.copy(dx[k][:], acc[:])
+            dx[pair] = ring.tile([P, PAIR], F32, name="dx", align_bytes=64)
+            nc.scalar.copy(dx[pair][:], sums[:])
 
-        def stage_scatter(k):
-            nc.vector.tensor_copy(window[:].indirect(offsets[:, k * PAIR // 16 : (k + 1) * PAIR // 16]), dx[k][:])
+        def stage_scatter(pair):
+            lo = pair * PAIR
+            nc.vector.tensor_copy(window[:].indirect(offsets_of(lo, lo + PAIR)), dx[pair][:])
+
+        gather(0, *GROUPS[1])
+        gather(0, *GROUPS[0])
+        gather(1, *GROUPS[0])
+        gather(1, *GROUPS[1])
+        gather(2, *GROUPS[0])
 
         stages = (
             (stage_gather, 0),
-            (stage_first, 1),
-            (stage_products, 2),
+            (stage_first_product, 1),
             (stage_saved, 1),
             (stage_mask, 3),
-            (stage_second, 3),
+            (stage_products, 2),
+            (stage_second_product, 3),
             (stage_scatter, 4),
         )
         for step in range(PAIRS + 4):

from contextlib import ExitStack

import concourse.mybir as mybir
from concourse.masks import make_identity

K, T, E, C, H = 128, 2048, 12, 128, 512
SLOTS = E * C
P = 128
PACK = 4
RUN = 4
PAIR = 2 * C
PAIRS = SLOTS // PAIR
OFFSETS_PER_COLUMN = 16

FLOPS = 2 * SLOTS * H * (H + 2 * K)

F32 = mybir.dt.float32
BF16 = mybir.dt.bfloat16
U32 = mybir.dt.uint32
I32 = mybir.dt.int32
U16 = mybir.dt.uint16
U8 = mybir.dt.uint8
FP8X4 = mybir.dt.float8_e4m3fn_x4
FP4X4 = mybir.dt.float4_e2m1fn_x4
MULT = mybir.AluOpType.mult
ACT = mybir.ActivationFunctionType

GROUPS = ((0, 512), (512, SLOTS))

SAVED_WIDTHS = (256, 256, 256, 256, 512)

W2_COUNTS = (2, 2, 4, 4)

GPSIMD_DA3_EXPERTS = (7, 9)


def tile_moe_bdx_glu_relu_kernel(
    tc, dyT, a1, a3, w2_words, w2_scales, w1_words, w1_scales, w3_words, w3_scales, gate, offs, out
):
    nc = tc.nc
    with ExitStack() as ctx:
        held = ctx.enter_context(tc.tile_pool(name="held", bufs=1))
        ring = ctx.enter_context(tc.tile_pool(name="ring", bufs=3))
        psum_dh = ctx.enter_context(tc.psum_pool(name="psum_dh", bufs=2))
        psum_turned = ctx.enter_context(tc.psum_pool(name="psum_turned", bufs=4))
        psum_dx = ctx.enter_context(tc.psum_pool(name="psum_dx", bufs=2))

        offsets = held.tile([P, SLOTS // OFFSETS_PER_COLUMN], U16, name="offsets")
        nc.sync.dma_start(offsets[:], offs)

        w2_s = held.tile([P, E, H], U8, name="w2_s", align_bytes=64)
        w1_s = held.tile([P, E, K], U8, name="w1_s", align_bytes=64)
        w3_s = held.tile([P, E, K], U8, name="w3_s", align_bytes=64)
        window = held.tile([P, T], F32, name="window", align_bytes=64)
        for scale_tile in (w2_s, w1_s, w3_s):
            nc.vector.memset(scale_tile[:].rearrange("p e n -> p (e n)").bitcast(I32), 0)
        nc.vector.memset(window[:], 0.0)
        identity = held.tile([P, P], F32, name="identity")
        make_identity(nc, identity[:])

        dy_rows = dyT.rearrange("(p d) t -> d p t", d=PACK)
        dy = [held.tile([P, T], F32, name="dy%d" % d, align_bytes=64) for d in range(PACK)]
        gates = [held.tile([P, hi - lo], F32, name="gate%d" % lo, align_bytes=64) for lo, hi in GROUPS]
        w2_w = [held.tile([P, n, 2 * H], U8, name="w2_w%d" % q, align_bytes=64) for q, n in enumerate(W2_COUNTS)]
        w1_w = held.tile([P, E, 2 * K], U8, name="w1_w", align_bytes=64)
        w3_w = held.tile([P, E, 2 * K], U8, name="w3_w", align_bytes=64)
        a1_in = [held.tile([P, PACK, n], F32, name="a1_in%d" % c, align_bytes=64) for c, n in enumerate(SAVED_WIDTHS)]
        a3_in = [held.tile([P, PACK, n], F32, name="a3_in%d" % c, align_bytes=64) for c, n in enumerate(SAVED_WIDTHS)]

        def load_scales(tile, source):
            rows = source.bitcast(I32)
            for quad in range(4):
                nc.sync.dma_start(
                    tile[32 * quad : 32 * quad + 4, :, :].bitcast(I32),
                    rows[:, :, 4 * quad : 4 * quad + 4, :].rearrange("e s f n -> f (e s) n"),
                )

        def load_words(tile, source):
            nc.sync.dma_start(tile[:].bitcast(I32), source.bitcast(I32).rearrange("e s p n -> p (e s) n"))

        def load_w2(q):
            first = sum(W2_COUNTS[:q])
            load_words(w2_w[q], w2_words[first : first + W2_COUNTS[q]])

        def load_saved(c):
            lo = sum(SAVED_WIDTHS[:c])
            for tile, source in ((a1_in[c], a1), (a3_in[c], a3)):
                rows = source.rearrange("(p t) s -> p t s", t=PACK)
                nc.sync.dma_start(tile[:], rows[:, :, lo : lo + SAVED_WIDTHS[c]])

        def load_gate(group):
            lo, hi = GROUPS[group]
            nc.sync.dma_start(gates[group][:], gate[0:P, lo:hi])

        nc.sync.dma_start(dy[0][:], dy_rows[0])
        load_gate(0)
        for d in range(1, PACK):
            nc.sync.dma_start(dy[d][:], dy_rows[d])
        load_scales(w2_s, w2_scales)
        load_w2(0)
        load_saved(0)
        load_gate(1)
        load_w2(1)
        load_scales(w1_s, w1_scales)
        load_scales(w3_s, w3_scales)
        load_words(w1_w, w1_words)
        load_words(w3_w, w3_words)
        load_saved(1)
        load_w2(2)
        load_saved(2)
        load_saved(3)
        load_w2(3)
        load_saved(4)

        w2_of = [w2_w[q][:, i, :] for q, n in enumerate(W2_COUNTS) for i in range(n)]

        gathered = [held.tile([P, PACK, hi - lo], F32, name="gathered%d" % lo, align_bytes=64) for lo, hi in GROUPS]

        def offsets_of(lo, hi):
            return offsets[:, lo // OFFSETS_PER_COLUMN : hi // OFFSETS_PER_COLUMN]

        def gather(d, lo, hi):
            looked_up = dy[d][:].indirect(offsets_of(lo, hi))
            if hi <= GROUPS[0][1]:
                nc.vector.tensor_tensor(gathered[0][:, d, lo:hi], looked_up, gates[0][:, lo:hi], MULT)
            else:
                first = GROUPS[1][0]
                nc.vector.tensor_copy(gathered[1][:, d, lo - first : hi - first], looked_up)

        def runs(block):
            return block.rearrange("p t (q i) -> p q t i", i=RUN)

        def runs_out(block):
            return block.rearrange("p (q i) t -> p q t i", i=RUN)

        def one_by_one(block):
            return block.rearrange("p t c -> p c t")

        g, g_codes, g_scales, turned = {}, {}, {}, {}
        relu, positive, da, da_codes, da_scales, dx = {}, {}, {}, {}, {}, {}

        def saved_of(tiles, pair):
            lo = pair * PAIR
            c = 0
            while lo >= SAVED_WIDTHS[c]:
                lo -= SAVED_WIDTHS[c]
                c += 1
            return tiles[c][:, :, lo : lo + PAIR]

        def stage_gather(pair):
            lo = pair * PAIR
            group = int(lo >= GROUPS[1][0])
            if group == 0:
                gather(3, lo, lo + PAIR)
            elif pair % 2 == 0:
                gather(2, lo, lo + 2 * PAIR)
                gather(3, lo, lo + 2 * PAIR)
            g[pair] = ring.tile([P, PAIR, PACK], BF16, name="g", align_bytes=64)
            lo -= GROUPS[group][0]
            if group == 0:
                nc.scalar.copy(runs_out(g[pair][:]), runs(gathered[0][:, :, lo : lo + PAIR]))
                return
            for j in range(2):
                cols = slice(lo + j * C, lo + (j + 1) * C)
                nc.gpsimd.tensor_tensor(
                    g[pair][:, j * C : (j + 1) * C, :],
                    one_by_one(gathered[1][:, :, cols]),
                    gates[1][:, cols].unsqueeze(2).to_broadcast([P, C, PACK]),
                    MULT,
                )

        def stage_first_product(pair):
            g_codes[pair] = ring.tile([P, PAIR], U32, name="g_codes", align_bytes=64)
            g_scales[pair] = ring.tile([P, PAIR], U8, name="g_scales", align_bytes=64)
            nc.vector.quantize_mx(
                out=g_codes[pair][:].bitcast(FP8X4),
                scales=g_scales[pair][:],
                in_=g[pair][:].rearrange("p s d -> p (s d)"),
            )
            for j in range(2):
                e = 2 * pair + j
                cols = slice(j * C, (j + 1) * C)
                dh = psum_dh.tile([P, H], F32, name="dh")
                nc.tensor.matmul_mx(
                    out=dh[:],
                    lhsT=g_codes[pair][:, cols].bitcast(FP8X4),
                    lhsT_scale=g_scales[pair][:, cols],
                    rhs=w2_of[e].bitcast(FP4X4),
                    rhs_scale=w2_s[:, e, :],
                    start=True,
                    stop=True,
                )
                dh_blocks = ring.tile([P, PACK, P], F32, name="dh_blocks", align_bytes=64)
                nc.scalar.copy(dh_blocks[:], dh[:].rearrange("p (m t) -> p t m", t=PACK))
                turned[e] = psum_turned.tile([P, PACK, C], F32, name="turned")
                for t in range(PACK):
                    nc.tensor.transpose(turned[e][:, t, :], dh_blocks[:, t, :], identity[:])

        def stage_saved(pair):
            relu[pair] = ring.tile([P, PACK, PAIR], F32, name="relu", align_bytes=64)
            nc.scalar.activation(relu[pair][:], saved_of(a1_in, pair), ACT.Relu)
            positive[pair] = ring.tile([P, PAIR, PACK], BF16, name="positive", align_bytes=64)
            nc.scalar.activation(runs_out(positive[pair][:]), runs(relu[pair][:]), ACT.Sign)

        def stage_products(pair):
            da[pair] = ring.tile([P, 2, 2, C, PACK], BF16, name="da", align_bytes=64)
            for which, factor in enumerate((saved_of(a3_in, pair), relu[pair][:])):
                for j in range(2):
                    e = 2 * pair + j
                    cols = slice(j * C, (j + 1) * C)
                    if which == 1 and e in GPSIMD_DA3_EXPERTS:
                        dh_copy = ring.tile([P, PACK, C], F32, name="dh_copy", align_bytes=64)
                        nc.scalar.copy(dh_copy[:], turned[e][:])
                        nc.gpsimd.tensor_tensor(
                            da[pair][:, which, j], one_by_one(dh_copy[:]), one_by_one(factor[:, :, cols]), MULT
                        )
                    else:
                        nc.vector.tensor_tensor(
                            runs_out(da[pair][:, which, j]), runs(turned[e][:]), runs(factor[:, :, cols]), MULT
                        )

        def stage_mask(pair):
            da1 = da[pair][:, 0].rearrange("p j c t -> p (j c t)")
            nc.vector.tensor_tensor(da1, da1, positive[pair][:].rearrange("p c t -> p (c t)"), MULT)

        def stage_second_product(pair):
            da_codes[pair] = ring.tile([P, 2, 2, C], U32, name="da_codes", align_bytes=64)
            da_scales[pair] = ring.tile([P, 2, 2, C], U8, name="da_scales", align_bytes=64)
            nc.vector.quantize_mx(
                out=da_codes[pair][:].rearrange("p w j c -> p (w j c)").bitcast(FP8X4),
                scales=da_scales[pair][:].rearrange("p w j c -> p (w j c)"),
                in_=da[pair][:].rearrange("p w j c t -> p (w j c t)"),
            )
            sums = psum_dx.tile([P, PAIR], F32, name="sums")
            for j in range(2):
                e = 2 * pair + j
                for which, (words, scales) in enumerate(((w1_w, w1_s), (w3_w, w3_s))):
                    nc.tensor.matmul_mx(
                        out=sums[:, j * C : (j + 1) * C],
                        lhsT=words[:, e, :].bitcast(FP4X4),
                        lhsT_scale=scales[:, e, :],
                        rhs=da_codes[pair][:, which, j, :].bitcast(FP8X4),
                        rhs_scale=da_scales[pair][:, which, j, :],
                        start=(which == 0),
                        stop=(which == 1),
                    )
            dx[pair] = ring.tile([P, PAIR], F32, name="dx", align_bytes=64)
            nc.scalar.copy(dx[pair][:], sums[:])

        def stage_scatter(pair):
            lo = pair * PAIR
            nc.vector.tensor_copy(window[:].indirect(offsets_of(lo, lo + PAIR)), dx[pair][:])

        gather(0, *GROUPS[1])
        gather(0, *GROUPS[0])
        gather(1, *GROUPS[0])
        gather(1, *GROUPS[1])
        gather(2, *GROUPS[0])

        stages = (
            (stage_gather, 0),
            (stage_first_product, 1),
            (stage_saved, 1),
            (stage_mask, 3),
            (stage_products, 2),
            (stage_second_product, 3),
            (stage_scatter, 4),
        )
        for step in range(PAIRS + 4):
            for stage, lag in stages:
                if 0 <= step - lag < PAIRS:
                    stage(step - lag)

        nc.sync.dma_start(out, window[:])
